import numpy as np
import ml_dtypes


def mxq(x, axis, fmt="e4m3"):
    dtype, down = {"e4m3": (ml_dtypes.float8_e4m3fn, 7), "e5m2": (ml_dtypes.float8_e5m2, 14)}[fmt]
    v = np.moveaxis(np.asarray(x, np.float32).astype(ml_dtypes.bfloat16).astype(np.float64), axis, -1)
    blocks = v.reshape(v.shape[:-1] + (-1, 32))
    amax = np.abs(blocks).max(-1, keepdims=True)
    byte = np.maximum(np.where(amax > 0, np.frexp(amax)[1] - 1 + 127, 0) - down, 1)
    scale = np.exp2(byte - 127.0)
    codes = (blocks / scale).astype(np.float32).astype(dtype).astype(np.float64)
    return np.moveaxis((codes * scale).reshape(v.shape), -1, axis)


WIDE = False


def mx_kscale(k):
    if not WIDE:
        return np.ones(k)
    levels = np.array([30, -30])
    if k % 512:
        return np.exp2(np.random.permutation(np.resize(levels, k // 32))).repeat(32)
    a = np.empty((k // 512, 16))
    for p in range(k // 512):
        a[p, :8] = np.random.permutation(np.resize(levels, 8))
        for g in range(8):
            far = levels[np.abs(levels - a[p, g]) >= 10]
            a[p, g + 8] = far[np.random.randint(len(far))]
    return np.exp2(a.ravel()).repeat(32)


BF16 = ml_dtypes.bfloat16


def bf(x):
    return np.asarray(x, np.float32).astype(BF16)


def f64(x):
    return np.asarray(x).astype(np.float64)


E2M1 = np.array([0.0, 0.5, 1.0, 1.5, 2.0, 3.0, 4.0, 6.0, -0.0, -0.5, -1.0, -1.5, -2.0, -3.0, -4.0, -6.0])


def pack_weight(w, fmt):
    k, n = w.shape
    w = f64(bf(w)).reshape(k // 32, 32, n)
    amax = np.abs(w).max(1)
    if fmt in ("e4m3", "e5m2"):
        byte = np.frexp(amax)[1] - 1 + 127 - (7 if fmt == "e4m3" else 14)
    else:
        mant, ex = np.frexp(amax / 6.0)
        byte = np.where(mant > 0.5, ex, ex - 1) + 127
    byte = np.clip(np.where(amax > 0, byte, 1), 1, 254)
    scaled = (w * np.exp2(127.0 - byte)[:, None, :]).reshape(k, n).astype(np.float32)
    by_word = np.ascontiguousarray(scaled.reshape(k // 512, 128, 4, n).transpose(0, 1, 3, 2))
    if fmt in ("e4m3", "e5m2"):
        words = by_word.astype(ml_dtypes.float8_e4m3fn if fmt == "e4m3" else ml_dtypes.float8_e5m2).view(np.uint8)
    else:
        c = by_word.astype(ml_dtypes.float4_e2m1fn).view(np.uint8) & 0xF
        words = c[..., 0::2] | (c[..., 1::2] << 4)
    return np.ascontiguousarray(words), np.ascontiguousarray(byte.astype(np.uint8).reshape(k // 512, 16, n))


def unpack_weight(words, scales, fmt):
    g, p, n, _ = words.shape
    if fmt in ("e4m3", "e5m2"):
        vals = np.ascontiguousarray(words).view(ml_dtypes.float8_e4m3fn if fmt == "e4m3" else ml_dtypes.float8_e5m2).astype(np.float64)
    else:
        nib = np.empty((g, p, n, 4), np.uint8)
        nib[..., 0::2] = words & 0xF
        nib[..., 1::2] = words >> 4
        vals = E2M1[nib]
    vals = vals * np.repeat(np.exp2(scales.astype(np.float64) - 127.0), 8, axis=1)[..., None]
    return vals.transpose(0, 1, 3, 2).reshape(g * 512, n)


T, H, C, D = 1024, 1536, 1024, 512
DOF = 5.0


def setup_inputs():
    s = mx_kscale(C)
    r = mx_kscale(D)
    G = np.random.standard_t(DOF, (C, T)) * np.sqrt((DOF - 2) / DOF) * s[:, None]
    g_words, g_scales = pack_weight(G, "e5m2")
    return {"g_words": g_words,
            "g_scales": g_scales,
            "w": bf(np.random.standard_normal((H, C)) / np.sqrt(C) / s),
            "a": bf(np.random.standard_normal((T, D)) * r),
            "v": bf(np.random.standard_normal((H, D)) / np.sqrt(D) / r),
            "lam": bf(np.exp(0.3 * np.random.standard_normal(T))),
            "gain": bf(1 + 0.1 * np.random.standard_normal(H))}


def reference(g_words, g_scales, w, a, v, lam, gain):
    G = unpack_weight(g_words, g_scales, "e5m2")
    wq = mxq(f64(w), 1, "e4m3")
    aq = mxq(f64(a), 1, "e4m3")
    vq = mxq(f64(v), 1, "e4m3")
    noise_part = G.T @ wq.T
    feature_part = aq @ vq.T
    dh = noise_part + feature_part
    return dh * f64(lam)[:, None] * f64(gain)

@@ -1,0 +1,313 @@
+from contextlib import ExitStack
+
+import concourse.mybir as mybir
+from concourse.masks import make_identity
+
+T, H, C, D = 1024, 1536, 1024, 512
+FLOPS = 2 * T * H * (C + D)
+
+F32 = mybir.dt.float32
+BF16 = mybir.dt.bfloat16
+I32 = mybir.dt.int32
+U32 = mybir.dt.uint32
+U8 = mybir.dt.uint8
+E4M3 = mybir.dt.float8_e4m3fn_x4
+E5M2 = mybir.dt.float8_e5m2_x4
+MULT = mybir.AluOpType.mult
+COPY = mybir.ActivationFunctionType.Copy
+
+P = 128
+NB = 512
+BLOCKS = H // NB
+TILES = T // P
+
+
+def tile_noise_error_backprop_e4_kernel(tc, g_words, g_scales, w, a, v, lam, gain, out):
+    nc = tc.nc
+    with ExitStack() as ctx:
+        keep = ctx.enter_context(tc.tile_pool(name="keep", bufs=1))
+        work = ctx.enter_context(tc.tile_pool(name="work", bufs=1))
+        psum = ctx.enter_context(tc.psum_pool(name="psum", bufs=1))
+        ctx.enter_context(tc.manual_schedule())
+
+        vec = keep.tile([P, P], BF16, name="vec")
+        ident = keep.tile([P, P], F32, name="ident")
+        ident_bf = keep.tile([P, P], BF16, name="ident_bf")
+        lam_sb = keep.tile([P, TILES], F32, name="lam_sb")
+        gain_cols = keep.tile([P, H // P], BF16, name="gain_cols")
+        gain_sb = [keep.tile([P, NB], BF16, name="gain_sb%d" % b) for b in range(BLOCKS)]
+        dummy = keep.tile([P, 1], F32, name="dummy")
+        g_raw = keep.tile([P, 2, T], U32, name="g_raw", align_bytes=64)
+        g_sc = keep.tile([P, 2, T], U8, name="g_sc", align_bytes=64)
+        a_raw = keep.tile([P, TILES, D], BF16, name="a_raw", align_bytes=64)
+        a_codes = keep.tile([P, T], U32, name="a_codes", align_bytes=64)
+        a_sc = keep.tile([P, T], U8, name="a_sc", align_bytes=64)
+        v_raw = [keep.tile([P, 4, D], BF16, name="v_raw%d" % b, align_bytes=64) for b in range(BLOCKS)]
+        w_raw = [keep.tile([P, 4, C], BF16, name="w_raw%d" % b, align_bytes=64) for b in range(BLOCKS)]
+        v_codes = [keep.tile([P, NB], U32, name="v_codes%d" % b, align_bytes=64) for b in range(BLOCKS)]
+        v_sc = [keep.tile([P, NB], U8, name="v_sc%d" % b, align_bytes=64) for b in range(BLOCKS)]
+        w_codes = [[keep.tile([P, NB], U32, name="w_codes%d_%d" % (b, g), align_bytes=64) for g in range(2)] for b in range(BLOCKS)]
+        w_sc = [[keep.tile([P, NB], U8, name="w_sc%d_%d" % (b, g), align_bytes=64) for g in range(2)] for b in range(BLOCKS)]
+        v_perm = {b: keep.tile([P, 4 * D // 2], F32, name="v_perm%d" % b, align_bytes=64) for b in (1, 2)}
+        w_perm = {(b, h): keep.tile([P, 2 * C // 2], F32, name="w_perm%d_%d" % (b, h), align_bytes=64) for b in (1, 2) for h in range(2)}
+
+        nc.vector.memset(vec[:], 0.0)
+        nc.vector.memset(g_sc[:].rearrange("p g n -> p (g n)").bitcast(I32), 0)
+        nc.vector.memset(dummy[:], 0.0)
+        nc.scalar.dma_start(out=vec[0:8, :], in_=lam.rearrange("(r c) -> r c", c=P))
+        gain_rows = gain.rearrange("(r c) -> r c", c=P)
+        nc.scalar.dma_start(out=vec[8:16, :], in_=gain_rows[0:8, :])
+        nc.scalar.dma_start(out=vec[16:20, :], in_=gain_rows[8:12, :])
+        nc.scalar.copy(out=dummy[:], in_=dummy[:])
+        make_identity(nc, ident[:])
+        nc.vector.tensor_copy(out=ident_bf[:], in_=ident[:])
+        for q in range(4):
+            nc.gpsimd.dma_start(
+                out=g_sc[32 * q : 32 * q + 4, :, :].bitcast(I32),
+                in_=g_scales[:, 4 * q : 4 * q + 4, :].rearrange("g r n -> r g n").bitcast(I32),
+            )
+
+        a_rows = a.rearrange("(i p) d -> p i d", p=P)
+        v_rows = v.rearrange("(b p a) d -> b p a d", b=BLOCKS, a=4)
+        w_rows = w.rearrange("(b p a) c -> b p a c", b=BLOCKS, a=4)
+        g_bytes = g_words.rearrange("g p n t -> p g (n t)")
+
+        def load_a(h):
+            nc.sync.dma_start(out=a_raw[:, 4 * h : 4 * h + 4, :], in_=a_rows[:, 4 * h : 4 * h + 4, :])
+
+        def load_g(h):
+            cols = slice(h * 512, h * 512 + 512)
+            bytes_ = slice(h * 2048, h * 2048 + 2048)
+            nc.sync.dma_start(out=g_raw[:, :, cols].bitcast(I32), in_=g_bytes[:, :, bytes_].bitcast(I32))
+
+        def load_w(b, h):
+            nc.sync.dma_start(out=w_raw[b][:, 2 * h : 2 * h + 2, :], in_=w_rows[b, :, 2 * h : 2 * h + 2, :])
+
+        for h in range(2):
+            nc.sync.dma_start(out=v_raw[0][:, 2 * h : 2 * h + 2, :], in_=v_rows[0, :, 2 * h : 2 * h + 2, :])
+        load_a(0)
+        load_w(0, 0)
+        load_w(0, 1)
+        load_a(1)
+        load_g(0)
+        load_g(1)
+        for b in (1, 2):
+            nc.sync.dma_start(out=v_raw[b][:], in_=v_rows[b])
+            load_w(b, 0)
+            load_w(b, 1)
+
+        v_words = [v_raw[b][:].rearrange("p a d -> p (a d)").bitcast(F32) for b in range(BLOCKS)]
+        w_words = [w_raw[b][:].rearrange("p a c -> p (a c)").bitcast(F32) for b in range(BLOCKS)]
+        a_words = a_raw[:].rearrange("p i d -> p (i d)").bitcast(F32)
+
+        def transposes(pieces):
+            bank = psum.tile([P, 512], F32, name="bank", tag="tr", bufs=4)
+            for j, (words, start, permuted) in enumerate(pieces):
+                for u in range(2):
+                    src = words[:, start + 128 * u : start + 128 * u + 128] if permuted else words[:, start + u : start + 256 : 2]
+                    nc.tensor.transpose(bank[:, (2 * j + u) * P : (2 * j + u + 1) * P], src, ident[:])
+            return bank
+
+        def copy_out(bank, on_scalar):
+            grouped = work.tile([P, 1024], BF16, name="grouped", tag="grouped", bufs=8, align_bytes=64)
+            dst = grouped[:].bitcast(F32).rearrange("p (a r u) -> p a r u", a=2, u=2)
+            src = bank[:].rearrange("p (a u r) -> p a r u", a=2, u=2)
+            if on_scalar:
+                nc.scalar.copy(out=dst, in_=src)
+            else:
+                nc.vector.tensor_copy(out=dst, in_=src)
+            return grouped
+
+        def quantise(grouped, codes, scales):
+            nc.vector.quantize_mx(out=codes.bitcast(E4M3), scales=scales, in_=grouped[:])
+
+        def v_tr(b, h):
+            if b == 0:
+                return transposes([(v_words[b], 256 * (2 * h + j), False) for j in range(2)])
+            return transposes([(v_perm[b], 256 * (2 * h + j), True) for j in range(2)])
+
+        def w_tr(b, h, g):
+            if b == 0:
+                return transposes([(w_words[b], 512 * (2 * h + j) + 256 * g, False) for j in range(2)])
+            return transposes([(w_perm[b, h], 512 * j + 256 * g, True) for j in range(2)])
+
+        def a_tr(m):
+            return transposes([(a_words, 256 * (2 * m + j), False) for j in range(2)])
+
+        def v_q(b, h, grouped):
+            cols = slice(256 * h, 256 * h + 256)
+            quantise(grouped, v_codes[b][:, cols], v_sc[b][:, cols])
+
+        def w_q(b, h, g, grouped):
+            cols = slice(256 * h, 256 * h + 256)
+            quantise(grouped, w_codes[b][g][:, cols], w_sc[b][g][:, cols])
+
+        def a_q(m, grouped):
+            cols = slice(256 * m, 256 * m + 256)
+            quantise(grouped, a_codes[:, cols], a_sc[:, cols])
+
+        def v_permute(b):
+            nc.scalar.copy(
+                out=v_perm[b][:].rearrange("p (x u q) -> p x u q", u=2, q=P),
+                in_=v_words[b].rearrange("p (x q u) -> p x u q", u=2, q=P),
+            )
+
+        def w_permute(b, h):
+            nc.scalar.copy(
+                out=w_perm[b, h][:].rearrange("p (x u q) -> p x u q", u=2, q=P),
+                in_=w_words[b][:, 1024 * h : 1024 * h + 1024].rearrange("p (x q u) -> p x u q", u=2, q=P),
+            )
+
+        accs = {}
+
+        def av(b, i):
+            acc = psum.tile([P, NB], F32, name="acc", tag="acc", bufs=4)
+            accs[b, i] = acc
+            rows = slice(P * i, P * i + P)
+            nc.tensor.matmul_mx(
+                out=acc[:],
+                lhsT=a_codes[:, rows].bitcast(E4M3),
+                lhsT_scale=a_sc[:, rows],
+                rhs=v_codes[b][:].bitcast(E4M3),
+                rhs_scale=v_sc[b][:],
+                start=True,
+                stop=False,
+            )
+
+        def gw(b, i):
+            acc = accs[b, i]
+            rows = slice(P * i, P * i + P)
+            for g in range(2):
+                nc.tensor.matmul_mx(
+                    out=acc[:],
+                    lhsT=g_raw[:, g, rows].bitcast(E5M2),
+                    lhsT_scale=g_sc[:, g, rows],
+                    rhs=w_codes[b][g][:].bitcast(E4M3),
+                    rhs_scale=w_sc[b][g][:],
+                    start=False,
+                    stop=(g == 1),
+                )
+
+        def finish(b, i):
+            res = work.tile([P, NB], F32, name="res", tag="res", bufs=24)
+            nc.vector.scalar_tensor_tensor(
+                out=res[:].rearrange("m (p a) -> m p a", a=4),
+                in0=accs[b, i][:].rearrange("m (a p) -> m p a", a=4),
+                scalar=lam_sb[:, i : i + 1],
+                in1=gain_sb[b][:].rearrange("m (p a) -> m p a", a=4),
+                op0=MULT,
+                op1=MULT,
+            )
+            nc.sync.dma_start(out=out[P * i : P * i + P, NB * b : NB * b + NB], in_=res[:])
+
+        def gain_spread(b):
+            bank = psum.tile([P, NB], BF16, name="gain_bank", tag="tr", bufs=4)
+            for j in range(4):
+                m = 4 * b + j
+                nc.tensor.transpose(bank[:, P * j : P * j + P], gain_cols[:, m : m + 1].to_broadcast([P, P]), ident_bf[:])
+            nc.scalar.copy(out=gain_sb[b][:], in_=bank[:])
+
+        b0 = v_tr(0, 0)
+        g0 = copy_out(b0, True)
+        b1 = v_tr(0, 1)
+        g1 = copy_out(b1, False)
+        vec_bank = psum.tile([P, P], BF16, name="vec_bank", tag="tr", bufs=4)
+        nc.tensor.transpose(vec_bank[:], vec[:], ident_bf[:])
+        v_q(0, 0, g0)
+        nc.scalar.copy(out=lam_sb[:], in_=vec_bank[:, 0:8])
+        nc.scalar.copy(out=gain_cols[:], in_=vec_bank[:, 8:20])
+        b2 = a_tr(0)
+        g2 = copy_out(b2, True)
+        b3 = a_tr(1)
+        g3 = copy_out(b3, False)
+        v_q(0, 1, g1)
+        a_q(0, g2)
+        a_q(1, g3)
+        gain_spread(0)
+        gs = {}
+        for h in range(2):
+            for g in range(2):
+                bank = w_tr(0, h, g)
+                gs[h, g] = copy_out(bank, g == 0)
+            if h == 0:
+                for i in range(4):
+                    av(0, i)
+            for g in range(2):
+                w_q(0, h, g, gs[h, g])
+        gain_spread(1)
+        b4 = a_tr(2)
+        g4 = copy_out(b4, True)
+        b5 = a_tr(3)
+        g5 = copy_out(b5, True)
+        gain_spread(2)
+        a_q(2, g4)
+        a_q(3, g5)
+
+        for i in range(4):
+            gw(0, i)
+            finish(0, i)
+        v_permute(1)
+        for i in (4, 5):
+            av(0, i)
+            gw(0, i)
+            finish(0, i)
+        w_permute(1, 0)
+        vb = [v_tr(1, 0), v_tr(1, 1)]
+        vg = [copy_out(bank, True) for bank in vb]
+        w_permute(1, 1)
+        wb = [w_tr(1, 0, g) for g in range(2)]
+        av(0, 6)
+        gw(0, 6)
+        wg = [copy_out(bank, True) for bank in wb]
+        for h in range(2):
+            v_q(1, h, vg[h])
+        finish(0, 6)
+        wb2 = [w_tr(1, 1, g) for g in range(2)]
+        av(0, 7)
+        gw(0, 7)
+        wg2 = [copy_out(bank, True) for bank in wb2]
+        for g in range(2):
+            w_q(1, 0, g, wg[g])
+        finish(0, 7)
+        v_permute(2)
+        vb = [v_tr(2, 0), v_tr(2, 1)]
+        for g in range(2):
+            w_q(1, 1, g, wg2[g])
+        vg = [copy_out(bank, True) for bank in vb]
+
+        for i in range(4):
+            av(1, i)
+        w_permute(2, 0)
+        gw(1, 0)
+        finish(1, 0)
+        for h in range(2):
+            v_q(2, h, vg[h])
+        for i in (1, 2):
+            gw(1, i)
+            finish(1, i)
+        wb = [w_tr(2, 0, g) for g in range(2)]
+        w_permute(2, 1)
+        wg = [copy_out(bank, True) for bank in wb]
+        gw(1, 3)
+        finish(1, 3)
+        av(1, 4)
+        gw(1, 4)
+        finish(1, 4)
+        for g in range(2):
+            w_q(2, 0, g, wg[g])
+        wb = [w_tr(2, 1, g) for g in range(2)]
+        wg = [copy_out(bank, True) for bank in wb]
+        av(1, 5)
+        gw(1, 5)
+        finish(1, 5)
+        for g in range(2):
+            w_q(2, 1, g, wg[g])
+        for i in (6, 7):
+            av(1, i)
+            gw(1, i)
+            finish(1, i)
+
+        for i in range(TILES):
+            av(2, i)
+            gw(2, i)
+            finish(2, i)

@@ -37,35 +37,31 @@ def tile_noise_error_backprop_e4_kernel(tc, g_words, g_scales, w, a, v, lam, gai
         gain_cols = keep.tile([P, H // P], BF16, name="gain_cols")
         gain_sb = [keep.tile([P, NB], BF16, name="gain_sb%d" % b) for b in range(BLOCKS)]
         dummy = keep.tile([P, 1], F32, name="dummy")
-        g_raw = keep.tile([P, 2, T], U32, name="g_raw", align_bytes=64)
+        g_raw = [keep.tile([P, 2, T // 2], U32, name="g_raw%d" % h, align_bytes=64) for h in range(2)]
         g_sc = keep.tile([P, 2, T], U8, name="g_sc", align_bytes=64)
         a_raw = keep.tile([P, TILES, D], BF16, name="a_raw", align_bytes=64)
         a_codes = keep.tile([P, T], U32, name="a_codes", align_bytes=64)
         a_sc = keep.tile([P, T], U8, name="a_sc", align_bytes=64)
         v_raw = [keep.tile([P, 4, D], BF16, name="v_raw%d" % b, align_bytes=64) for b in range(BLOCKS)]
+        w_first = [keep.tile([P, 2, C // 2], BF16, name="w_first%d" % g, align_bytes=64) for g in range(2)]
         w_raw = [keep.tile([P, 4, C], BF16, name="w_raw%d" % b, align_bytes=64) for b in range(BLOCKS)]
         v_codes = [keep.tile([P, NB], U32, name="v_codes%d" % b, align_bytes=64) for b in range(BLOCKS)]
         v_sc = [keep.tile([P, NB], U8, name="v_sc%d" % b, align_bytes=64) for b in range(BLOCKS)]
         w_codes = [[keep.tile([P, NB], U32, name="w_codes%d_%d" % (b, g), align_bytes=64) for g in range(2)] for b in range(BLOCKS)]
         w_sc = [[keep.tile([P, NB], U8, name="w_sc%d_%d" % (b, g), align_bytes=64) for g in range(2)] for b in range(BLOCKS)]
         v_perm = {b: keep.tile([P, 4 * D // 2], F32, name="v_perm%d" % b, align_bytes=64) for b in (1, 2)}
+        a_perm = keep.tile([P, 4 * D // 2], F32, name="a_perm", align_bytes=64)
         w_perm = {(b, h): keep.tile([P, 2 * C // 2], F32, name="w_perm%d_%d" % (b, h), align_bytes=64) for b in (1, 2) for h in range(2)}
 
         nc.vector.memset(vec[:], 0.0)
         nc.vector.memset(g_sc[:].rearrange("p g n -> p (g n)").bitcast(I32), 0)
         nc.vector.memset(dummy[:], 0.0)
+        make_identity(nc, ident[:])
         nc.scalar.dma_start(out=vec[0:8, :], in_=lam.rearrange("(r c) -> r c", c=P))
         gain_rows = gain.rearrange("(r c) -> r c", c=P)
-        nc.scalar.dma_start(out=vec[8:16, :], in_=gain_rows[0:8, :])
-        nc.scalar.dma_start(out=vec[16:20, :], in_=gain_rows[8:12, :])
+        nc.scalar.dma_start(out=vec[8:20, :], in_=gain_rows)
         nc.scalar.copy(out=dummy[:], in_=dummy[:])
-        make_identity(nc, ident[:])
         nc.vector.tensor_copy(out=ident_bf[:], in_=ident[:])
-        for q in range(4):
-            nc.gpsimd.dma_start(
-                out=g_sc[32 * q : 32 * q + 4, :, :].bitcast(I32),
-                in_=g_scales[:, 4 * q : 4 * q + 4, :].rearrange("g r n -> r g n").bitcast(I32),
-            )
 
         a_rows = a.rearrange("(i p) d -> p i d", p=P)
         v_rows = v.rearrange("(b p a) d -> b p a d", b=BLOCKS, a=4)
@@ -76,20 +72,25 @@ def tile_noise_error_backprop_e4_kernel(tc, g_words, g_scales, w, a, v, lam, gai
             nc.sync.dma_start(out=a_raw[:, 4 * h : 4 * h + 4, :], in_=a_rows[:, 4 * h : 4 * h + 4, :])
 
         def load_g(h):
-            cols = slice(h * 512, h * 512 + 512)
             bytes_ = slice(h * 2048, h * 2048 + 2048)
-            nc.sync.dma_start(out=g_raw[:, :, cols].bitcast(I32), in_=g_bytes[:, :, bytes_].bitcast(I32))
+            nc.sync.dma_start(out=g_raw[h][:].bitcast(I32), in_=g_bytes[:, :, bytes_].bitcast(I32))
 
         def load_w(b, h):
             nc.sync.dma_start(out=w_raw[b][:, 2 * h : 2 * h + 2, :], in_=w_rows[b, :, 2 * h : 2 * h + 2, :])
 
-        for h in range(2):
-            nc.sync.dma_start(out=v_raw[0][:, 2 * h : 2 * h + 2, :], in_=v_rows[0, :, 2 * h : 2 * h + 2, :])
-        load_a(0)
-        load_w(0, 0)
+        for g in range(2):
+            cols = slice(g * 512, g * 512 + 512)
+            nc.sync.dma_start(out=w_first[g][:], in_=w_rows[0, :, 0:2, cols])
         load_w(0, 1)
-        load_a(1)
+        nc.sync.dma_start(out=v_raw[0][:], in_=v_rows[0])
+        for q in range(4):
+            nc.sync.dma_start(
+                out=g_sc[32 * q : 32 * q + 4, :, :].bitcast(I32),
+                in_=g_scales[:, 4 * q : 4 * q + 4, :].rearrange("g r n -> r g n").bitcast(I32),
+            )
+        load_a(0)
         load_g(0)
+        load_a(1)
         load_g(1)
         for b in (1, 2):
             nc.sync.dma_start(out=v_raw[b][:], in_=v_rows[b])
@@ -98,6 +99,7 @@ def tile_noise_error_backprop_e4_kernel(tc, g_words, g_scales, w, a, v, lam, gai
 
         v_words = [v_raw[b][:].rearrange("p a d -> p (a d)").bitcast(F32) for b in range(BLOCKS)]
         w_words = [w_raw[b][:].rearrange("p a c -> p (a c)").bitcast(F32) for b in range(BLOCKS)]
+        w_first_words = [w_first[g][:].rearrange("p a c -> p (a c)").bitcast(F32) for g in range(2)]
         a_words = a_raw[:].rearrange("p i d -> p (i d)").bitcast(F32)
 
         def transposes(pieces):
@@ -127,12 +129,16 @@ def tile_noise_error_backprop_e4_kernel(tc, g_words, g_scales, w, a, v, lam, gai
             return transposes([(v_perm[b], 256 * (2 * h + j), True) for j in range(2)])
 
         def w_tr(b, h, g):
+            if b == 0 and h == 0:
+                return transposes([(w_first_words[g], 256 * j, False) for j in range(2)])
             if b == 0:
                 return transposes([(w_words[b], 512 * (2 * h + j) + 256 * g, False) for j in range(2)])
             return transposes([(w_perm[b, h], 512 * j + 256 * g, True) for j in range(2)])
 
         def a_tr(m):
-            return transposes([(a_words, 256 * (2 * m + j), False) for j in range(2)])
+            if m < 2:
+                return transposes([(a_words, 256 * (2 * m + j), False) for j in range(2)])
+            return transposes([(a_perm, 256 * (2 * (m - 2) + j), True) for j in range(2)])
 
         def v_q(b, h, grouped):
             cols = slice(256 * h, 256 * h + 256)
@@ -146,59 +152,70 @@ def tile_noise_error_backprop_e4_kernel(tc, g_words, g_scales, w, a, v, lam, gai
             cols = slice(256 * m, 256 * m + 256)
             quantise(grouped, a_codes[:, cols], a_sc[:, cols])
 
-        def v_permute(b):
-            nc.scalar.copy(
-                out=v_perm[b][:].rearrange("p (x u q) -> p x u q", u=2, q=P),
-                in_=v_words[b].rearrange("p (x q u) -> p x u q", u=2, q=P),
-            )
+        def permute(dst, src, on_scalar):
+            dst = dst.rearrange("p (x u q) -> p x u q", u=2, q=P)
+            src = src.rearrange("p (x q u) -> p x u q", u=2, q=P)
+            if on_scalar:
+                nc.scalar.copy(out=dst, in_=src)
+            else:
+                nc.vector.tensor_copy(out=dst, in_=src)
 
-        def w_permute(b, h):
-            nc.scalar.copy(
-                out=w_perm[b, h][:].rearrange("p (x u q) -> p x u q", u=2, q=P),
-                in_=w_words[b][:, 1024 * h : 1024 * h + 1024].rearrange("p (x q u) -> p x u q", u=2, q=P),
-            )
+        def a_permute(on_scalar):
+            permute(a_perm[:], a_words[:, 1024:2048], on_scalar)
+
+        def v_permute(b, on_scalar):
+            permute(v_perm[b][:], v_words[b], on_scalar)
+
+        def w_permute(b, h, on_scalar):
+            permute(w_perm[b, h][:], w_words[b][:, 1024 * h : 1024 * h + 1024], on_scalar)
 
         accs = {}
 
-        def av(b, i):
+        def open_acc(b, i):
             acc = psum.tile([P, NB], F32, name="acc", tag="acc", bufs=4)
             accs[b, i] = acc
+
+        def av(b, i, start, stop):
             rows = slice(P * i, P * i + P)
             nc.tensor.matmul_mx(
-                out=acc[:],
+                out=accs[b, i][:],
                 lhsT=a_codes[:, rows].bitcast(E4M3),
                 lhsT_scale=a_sc[:, rows],
                 rhs=v_codes[b][:].bitcast(E4M3),
                 rhs_scale=v_sc[b][:],
-                start=True,
-                stop=False,
+                start=start,
+                stop=stop,
             )
 
-        def gw(b, i):
-            acc = accs[b, i]
+        def gw(b, i, start, stop):
             rows = slice(P * i, P * i + P)
+            words = slice(P * (i % 4), P * (i % 4) + P)
             for g in range(2):
                 nc.tensor.matmul_mx(
-                    out=acc[:],
-                    lhsT=g_raw[:, g, rows].bitcast(E5M2),
+                    out=accs[b, i][:],
+                    lhsT=g_raw[i // 4][:, g, words].bitcast(E5M2),
                     lhsT_scale=g_sc[:, g, rows],
                     rhs=w_codes[b][g][:].bitcast(E4M3),
                     rhs_scale=w_sc[b][g][:],
-                    start=False,
-                    stop=(g == 1),
+                    start=start and g == 0,
+                    stop=stop and g == 1,
                 )
 
         def finish(b, i):
             res = work.tile([P, NB], F32, name="res", tag="res", bufs=24)
-            nc.vector.scalar_tensor_tensor(
-                out=res[:].rearrange("m (p a) -> m p a", a=4),
-                in0=accs[b, i][:].rearrange("m (a p) -> m p a", a=4),
-                scalar=lam_sb[:, i : i + 1],
-                in1=gain_sb[b][:].rearrange("m (p a) -> m p a", a=4),
-                op0=MULT,
-                op1=MULT,
-            )
-            nc.sync.dma_start(out=out[P * i : P * i + P, NB * b : NB * b + NB], in_=res[:])
+            pieces = 2 if (b, i) == (BLOCKS - 1, TILES - 1) else 1
+            n = P // pieces
+            for s in range(pieces):
+                cols = slice(4 * n * s, 4 * n * (s + 1))
+                nc.vector.scalar_tensor_tensor(
+                    out=res[:, cols].rearrange("m (p a) -> m p a", a=4),
+                    in0=accs[b, i][:].rearrange("m (a p) -> m p a", a=4)[:, n * s : n * (s + 1), :],
+                    scalar=lam_sb[:, i : i + 1],
+                    in1=gain_sb[b][:, cols].rearrange("m (p a) -> m p a", a=4),
+                    op0=MULT,
+                    op1=MULT,
+                )
+                nc.sync.dma_start(out=out[P * i : P * i + P, NB * b + 4 * n * s : NB * b + 4 * n * (s + 1)], in_=res[:, cols])
 
         def gain_spread(b):
             bank = psum.tile([P, NB], BF16, name="gain_bank", tag="tr", bufs=4)
@@ -207,107 +224,91 @@ def tile_noise_error_backprop_e4_kernel(tc, g_words, g_scales, w, a, v, lam, gai
                 nc.tensor.transpose(bank[:, P * j : P * j + P], gain_cols[:, m : m + 1].to_broadcast([P, P]), ident_bf[:])
             nc.scalar.copy(out=gain_sb[b][:], in_=bank[:])
 
-        b0 = v_tr(0, 0)
-        g0 = copy_out(b0, True)
-        b1 = v_tr(0, 1)
-        g1 = copy_out(b1, False)
+        def copies(banks, on_scalar):
+            return [copy_out(bank, s) for bank, s in zip(banks, on_scalar)]
+
+        def tile_av_first(b, i):
+            open_acc(b, i)
+            av(b, i, True, False)
+            gw(b, i, False, True)
+            finish(b, i)
+
         vec_bank = psum.tile([P, P], BF16, name="vec_bank", tag="tr", bufs=4)
         nc.tensor.transpose(vec_bank[:], vec[:], ident_bf[:])
-        v_q(0, 0, g0)
-        nc.scalar.copy(out=lam_sb[:], in_=vec_bank[:, 0:8])
         nc.scalar.copy(out=gain_cols[:], in_=vec_bank[:, 8:20])
-        b2 = a_tr(0)
-        g2 = copy_out(b2, True)
-        b3 = a_tr(1)
-        g3 = copy_out(b3, False)
-        v_q(0, 1, g1)
-        a_q(0, g2)
-        a_q(1, g3)
-        gain_spread(0)
-        gs = {}
-        for h in range(2):
-            for g in range(2):
-                bank = w_tr(0, h, g)
-                gs[h, g] = copy_out(bank, g == 0)
-            if h == 0:
-                for i in range(4):
-                    av(0, i)
-            for g in range(2):
-                w_q(0, h, g, gs[h, g])
-        gain_spread(1)
-        b4 = a_tr(2)
-        g4 = copy_out(b4, True)
-        b5 = a_tr(3)
-        g5 = copy_out(b5, True)
-        gain_spread(2)
-        a_q(2, g4)
-        a_q(3, g5)
-
+        nc.scalar.copy(out=lam_sb[:], in_=vec_bank[:, 0:8])
+        for b in range(BLOCKS):
+            gain_spread(b)
+        bank = w_tr(0, 0, 0)
+        w00 = copy_out(bank, True)
+        bank = w_tr(0, 0, 1)
+        w01 = copy_out(bank, False)
+        w_q(0, 0, 0, w00)
+        w_q(0, 0, 1, w01)
+        bank = w_tr(0, 1, 0)
+        w10 = copy_out(bank, True)
+        bank = w_tr(0, 1, 1)
+        w11 = copy_out(bank, False)
+        w_q(0, 1, 0, w10)
+        w_q(0, 1, 1, w11)
+        bank = v_tr(0, 0)
+        v0 = copy_out(bank, True)
+        bank = v_tr(0, 1)
+        v1 = copy_out(bank, True)
+        v_q(0, 0, v0)
+        bank = a_tr(0)
+        a0 = copy_out(bank, True)
+        bank = a_tr(1)
+        v_q(0, 1, v1)
+        a1 = copy_out(bank, False)
         for i in range(4):
-            gw(0, i)
+            open_acc(0, i)
+            gw(0, i, True, False)
+        a_q(0, a0)
+        a_q(1, a1)
+        a_permute(True)
+        v_permute(1, False)
+        a23 = copies([a_tr(2), a_tr(3)], [True, True])
+        a_q(2, a23[0])
+        w_permute(1, 0, False)
+        for i in range(4):
+            av(0, i, False, True)
             finish(0, i)
-        v_permute(1)
-        for i in (4, 5):
-            av(0, i)
-            gw(0, i)
-            finish(0, i)
-        w_permute(1, 0)
-        vb = [v_tr(1, 0), v_tr(1, 1)]
-        vg = [copy_out(bank, True) for bank in vb]
-        w_permute(1, 1)
-        wb = [w_tr(1, 0, g) for g in range(2)]
-        av(0, 6)
-        gw(0, 6)
-        wg = [copy_out(bank, True) for bank in wb]
-        for h in range(2):
-            v_q(1, h, vg[h])
-        finish(0, 6)
-        wb2 = [w_tr(1, 1, g) for g in range(2)]
-        av(0, 7)
-        gw(0, 7)
-        wg2 = [copy_out(bank, True) for bank in wb2]
+            if i == 0:
+                a_q(3, a23[1])
+        vg = copies([v_tr(1, 0), v_tr(1, 1)], [True, True])
+        w_permute(1, 1, True)
+        v_q(1, 0, vg[0])
+        v_q(1, 1, vg[1])
+        wg = copies([w_tr(1, 0, g) for g in range(2)], [True, True])
+        tile_av_first(0, 4)
+        v_permute(2, True)
         for g in range(2):
             w_q(1, 0, g, wg[g])
-        finish(0, 7)
-        v_permute(2)
-        vb = [v_tr(2, 0), v_tr(2, 1)]
+        wg2 = copies([w_tr(1, 1, g) for g in range(2)], [True, True])
+        tile_av_first(0, 5)
         for g in range(2):
             w_q(1, 1, g, wg2[g])
-        vg = [copy_out(bank, True) for bank in vb]
-
-        for i in range(4):
-            av(1, i)
-        w_permute(2, 0)
-        gw(1, 0)
-        finish(1, 0)
+        w_permute(2, 0, True)
+        tile_av_first(0, 6)
+        vg = copies([v_tr(2, 0), v_tr(2, 1)], [True, True])
+        tile_av_first(0, 7)
+        w_permute(2, 1, True)
         for h in range(2):
             v_q(2, h, vg[h])
-        for i in (1, 2):
-            gw(1, i)
-            finish(1, i)
-        wb = [w_tr(2, 0, g) for g in range(2)]
-        w_permute(2, 1)
-        wg = [copy_out(bank, True) for bank in wb]
-        gw(1, 3)
-        finish(1, 3)
-        av(1, 4)
-        gw(1, 4)
-        finish(1, 4)
+
+        tile_av_first(1, 0)
+        wg = copies([w_tr(2, 0, g) for g in range(2)], [True, True])
+        tile_av_first(1, 1)
         for g in range(2):
             w_q(2, 0, g, wg[g])
-        wb = [w_tr(2, 1, g) for g in range(2)]
-        wg = [copy_out(bank, True) for bank in wb]
-        av(1, 5)
-        gw(1, 5)
-        finish(1, 5)
+        tile_av_first(1, 2)
+        wg2 = copies([w_tr(2, 1, g) for g in range(2)], [True, True])
+        tile_av_first(1, 3)
         for g in range(2):
-            w_q(2, 1, g, wg[g])
-        for i in (6, 7):
-            av(1, i)
-            gw(1, i)
-            finish(1, i)
+            w_q(2, 1, g, wg2[g])
+        for i in range(4, TILES):
+            tile_av_first(1, i)
 
         for i in range(TILES):
-            av(2, i)
-            gw(2, i)
-            finish(2, i)
+            tile_av_first(2, i)

@@ -59,7 +59,8 @@ def tile_noise_error_backprop_e4_kernel(tc, g_words, g_scales, w, a, v, lam, gai
         make_identity(nc, ident[:])
         nc.scalar.dma_start(out=vec[0:8, :], in_=lam.rearrange("(r c) -> r c", c=P))
         gain_rows = gain.rearrange("(r c) -> r c", c=P)
-        nc.scalar.dma_start(out=vec[8:20, :], in_=gain_rows)
+        nc.scalar.dma_start(out=vec[8:16, :], in_=gain_rows[0:8, :])
+        nc.scalar.dma_start(out=vec[16:20, :], in_=gain_rows[8:12, :])
         nc.scalar.copy(out=dummy[:], in_=dummy[:])
         nc.vector.tensor_copy(out=ident_bf[:], in_=ident[:])
 
@@ -88,8 +89,9 @@ def tile_noise_error_backprop_e4_kernel(tc, g_words, g_scales, w, a, v, lam, gai
                 out=g_sc[32 * q : 32 * q + 4, :, :].bitcast(I32),
                 in_=g_scales[:, 4 * q : 4 * q + 4, :].rearrange("g r n -> r g n").bitcast(I32),
             )
-        load_a(0)
         load_g(0)
+        for m in range(2):
+            nc.sync.dma_start(out=a_raw[:, 2 * m : 2 * m + 2, :], in_=a_rows[:, 2 * m : 2 * m + 2, :])
         load_a(1)
         load_g(1)
         for b in (1, 2):
@@ -233,81 +235,70 @@ def tile_noise_error_backprop_e4_kernel(tc, g_words, g_scales, w, a, v, lam, gai
             gw(b, i, False, True)
             finish(b, i)
 
+        w00 = copies([w_tr(0, 0, 0), w_tr(0, 0, 1)], [False, False])
         vec_bank = psum.tile([P, P], BF16, name="vec_bank", tag="tr", bufs=4)
         nc.tensor.transpose(vec_bank[:], vec[:], ident_bf[:])
         nc.scalar.copy(out=gain_cols[:], in_=vec_bank[:, 8:20])
         nc.scalar.copy(out=lam_sb[:], in_=vec_bank[:, 0:8])
-        for b in range(BLOCKS):
-            gain_spread(b)
-        bank = w_tr(0, 0, 0)
-        w00 = copy_out(bank, True)
-        bank = w_tr(0, 0, 1)
-        w01 = copy_out(bank, False)
-        w_q(0, 0, 0, w00)
-        w_q(0, 0, 1, w01)
-        bank = w_tr(0, 1, 0)
-        w10 = copy_out(bank, True)
-        bank = w_tr(0, 1, 1)
-        w11 = copy_out(bank, False)
-        w_q(0, 1, 0, w10)
-        w_q(0, 1, 1, w11)
-        bank = v_tr(0, 0)
-        v0 = copy_out(bank, True)
-        bank = v_tr(0, 1)
-        v1 = copy_out(bank, True)
-        v_q(0, 0, v0)
-        bank = a_tr(0)
-        a0 = copy_out(bank, True)
-        bank = a_tr(1)
-        v_q(0, 1, v1)
-        a1 = copy_out(bank, False)
-        for i in range(4):
+        w01 = copies([w_tr(0, 1, 0), w_tr(0, 1, 1)], [True, False])
+        w_q(0, 0, 0, w00[0])
+        w_q(0, 0, 1, w00[1])
+        gain_spread(0)
+        w_q(0, 1, 0, w01[0])
+        w_q(0, 1, 1, w01[1])
+        v0 = copies([v_tr(0, 0), v_tr(0, 1)], [False, True])
+        v_q(0, 0, v0[0])
+        a0 = copies([a_tr(0), a_tr(1)], [True, False])
+        v_q(0, 1, v0[1])
+        open_acc(0, 0)
+        gw(0, 0, True, False)
+        a_permute(True)
+        a_q(0, a0[0])
+        gain_spread(1)
+        gain_spread(2)
+        a_q(1, a0[1])
+        a1 = copies([a_tr(2), a_tr(3)], [True, True])
+        for i in range(1, 4):
             open_acc(0, i)
             gw(0, i, True, False)
-        a_q(0, a0)
-        a_q(1, a1)
-        a_permute(True)
-        v_permute(1, False)
-        a23 = copies([a_tr(2), a_tr(3)], [True, True])
-        a_q(2, a23[0])
+        v_permute(1, True)
         w_permute(1, 0, False)
         for i in range(4):
             av(0, i, False, True)
             finish(0, i)
-            if i == 0:
-                a_q(3, a23[1])
+            if i < 2:
+                a_q(2 + i, a1[i])
         vg = copies([v_tr(1, 0), v_tr(1, 1)], [True, True])
+        wg = copies([w_tr(1, 0, g) for g in range(2)], [True, False])
         w_permute(1, 1, True)
+        v_permute(2, False)
+        tile_av_first(0, 4)
         v_q(1, 0, vg[0])
         v_q(1, 1, vg[1])
-        wg = copies([w_tr(1, 0, g) for g in range(2)], [True, True])
-        tile_av_first(0, 4)
-        v_permute(2, True)
-        for g in range(2):
-            w_q(1, 0, g, wg[g])
-        wg2 = copies([w_tr(1, 1, g) for g in range(2)], [True, True])
         tile_av_first(0, 5)
         for g in range(2):
-            w_q(1, 1, g, wg2[g])
-        w_permute(2, 0, True)
-        tile_av_first(0, 6)
+            w_q(1, 0, g, wg[g])
+        wg = copies([w_tr(1, 1, g) for g in range(2)], [True, True])
         vg = copies([v_tr(2, 0), v_tr(2, 1)], [True, True])
+        w_permute(2, 0, False)
+        w_permute(2, 1, False)
+        tile_av_first(0, 6)
+        for g in range(2):
+            w_q(1, 1, g, wg[g])
         tile_av_first(0, 7)
-        w_permute(2, 1, True)
         for h in range(2):
             v_q(2, h, vg[h])
 
+        wb = [w_tr(2, h, g) for h in range(2) for g in range(2)]
+        wg = copies(wb, [True] * 4)
         tile_av_first(1, 0)
-        wg = copies([w_tr(2, 0, g) for g in range(2)], [True, True])
         tile_av_first(1, 1)
         for g in range(2):
             w_q(2, 0, g, wg[g])
         tile_av_first(1, 2)
-        wg2 = copies([w_tr(2, 1, g) for g in range(2)], [True, True])
-        tile_av_first(1, 3)
         for g in range(2):
-            w_q(2, 1, g, wg2[g])
-        for i in range(4, TILES):
+            w_q(2, 1, g, wg[2 + g])
+        for i in range(3, TILES):
             tile_av_first(1, i)
 
         for i in range(TILES):

@@ -39,23 +39,28 @@ def tile_noise_error_backprop_e4_kernel(tc, g_words, g_scales, w, a, v, lam, gai
         dummy = keep.tile([P, 1], F32, name="dummy")
         g_raw = [keep.tile([P, 2, T // 2], U32, name="g_raw%d" % h, align_bytes=64) for h in range(2)]
         g_sc = keep.tile([P, 2, T], U8, name="g_sc", align_bytes=64)
-        a_raw = keep.tile([P, TILES, D], BF16, name="a_raw", align_bytes=64)
+        a_raw = keep.tile([P, TILES // 2, 2 * D], BF16, name="a_raw", align_bytes=64)
         a_codes = keep.tile([P, T], U32, name="a_codes", align_bytes=64)
         a_sc = keep.tile([P, T], U8, name="a_sc", align_bytes=64)
         v_raw = [keep.tile([P, 4, D], BF16, name="v_raw%d" % b, align_bytes=64) for b in range(BLOCKS)]
-        w_first = [keep.tile([P, 2, C // 2], BF16, name="w_first%d" % g, align_bytes=64) for g in range(2)]
+        w_first = [keep.tile([P, C], BF16, name="w_first%d" % s, align_bytes=64) for s in range(2)]
         w_raw = [keep.tile([P, 4, C], BF16, name="w_raw%d" % b, align_bytes=64) for b in range(BLOCKS)]
         v_codes = [keep.tile([P, NB], U32, name="v_codes%d" % b, align_bytes=64) for b in range(BLOCKS)]
         v_sc = [keep.tile([P, NB], U8, name="v_sc%d" % b, align_bytes=64) for b in range(BLOCKS)]
         w_codes = [[keep.tile([P, NB], U32, name="w_codes%d_%d" % (b, g), align_bytes=64) for g in range(2)] for b in range(BLOCKS)]
         w_sc = [[keep.tile([P, NB], U8, name="w_sc%d_%d" % (b, g), align_bytes=64) for g in range(2)] for b in range(BLOCKS)]
         v_perm = {b: keep.tile([P, 4 * D // 2], F32, name="v_perm%d" % b, align_bytes=64) for b in (1, 2)}
-        a_perm = keep.tile([P, 4 * D // 2], F32, name="a_perm", align_bytes=64)
+        a_perm = [keep.tile([P, 4 * D // 2], F32, name="a_perm%d" % h, align_bytes=64) for h in range(2)]
         w_perm = {(b, h): keep.tile([P, 2 * C // 2], F32, name="w_perm%d_%d" % (b, h), align_bytes=64) for b in (1, 2) for h in range(2)}
 
-        nc.vector.memset(vec[:], 0.0)
-        nc.vector.memset(g_sc[:].rearrange("p g n -> p (g n)").bitcast(I32), 0)
+        warm_in = keep.tile([P, 4 * NB], BF16, name="warm_in", align_bytes=64)
+        warm_codes = keep.tile([P, NB], U32, name="warm_codes", align_bytes=64)
+        warm_sc = keep.tile([P, NB], U8, name="warm_sc", align_bytes=64)
         nc.vector.memset(dummy[:], 0.0)
+        nc.vector.memset(warm_in[:].bitcast(F32), 0.0)
+        nc.gpsimd.memset(vec[:], 0.0)
+        nc.vector.quantize_mx(out=warm_codes[:].bitcast(E4M3), scales=warm_sc[:], in_=warm_in[:])
+        nc.vector.memset(g_sc[:].rearrange("p g n -> p (g n)").bitcast(I32), 0)
         make_identity(nc, ident[:])
         nc.scalar.dma_start(out=vec[0:8, :], in_=lam.rearrange("(r c) -> r c", c=P))
         gain_rows = gain.rearrange("(r c) -> r c", c=P)
@@ -64,13 +69,13 @@ def tile_noise_error_backprop_e4_kernel(tc, g_words, g_scales, w, a, v, lam, gai
         nc.scalar.copy(out=dummy[:], in_=dummy[:])
         nc.vector.tensor_copy(out=ident_bf[:], in_=ident[:])
 
-        a_rows = a.rearrange("(i p) d -> p i d", p=P)
+        a_rows = a.rearrange("(m p j) d -> p m (j d)", p=P, j=2)
         v_rows = v.rearrange("(b p a) d -> b p a d", b=BLOCKS, a=4)
         w_rows = w.rearrange("(b p a) c -> b p a c", b=BLOCKS, a=4)
         g_bytes = g_words.rearrange("g p n t -> p g (n t)")
 
-        def load_a(h):
-            nc.sync.dma_start(out=a_raw[:, 4 * h : 4 * h + 4, :], in_=a_rows[:, 4 * h : 4 * h + 4, :])
+        def load_a(m, n):
+            nc.sync.dma_start(out=a_raw[:, m : m + n, :], in_=a_rows[:, m : m + n, :])
 
         def load_g(h):
             bytes_ = slice(h * 2048, h * 2048 + 2048)
@@ -79,9 +84,8 @@ def tile_noise_error_backprop_e4_kernel(tc, g_words, g_scales, w, a, v, lam, gai
         def load_w(b, h):
             nc.sync.dma_start(out=w_raw[b][:, 2 * h : 2 * h + 2, :], in_=w_rows[b, :, 2 * h : 2 * h + 2, :])
 
-        for g in range(2):
-            cols = slice(g * 512, g * 512 + 512)
-            nc.sync.dma_start(out=w_first[g][:], in_=w_rows[0, :, 0:2, cols])
+        for s in range(2):
+            nc.sync.dma_start(out=w_first[s][:], in_=w_rows[0, :, s, :])
         load_w(0, 1)
         nc.sync.dma_start(out=v_raw[0][:], in_=v_rows[0])
         for q in range(4):
@@ -90,9 +94,8 @@ def tile_noise_error_backprop_e4_kernel(tc, g_words, g_scales, w, a, v, lam, gai
                 in_=g_scales[:, 4 * q : 4 * q + 4, :].rearrange("g r n -> r g n").bitcast(I32),
             )
         load_g(0)
-        for m in range(2):
-            nc.sync.dma_start(out=a_raw[:, 2 * m : 2 * m + 2, :], in_=a_rows[:, 2 * m : 2 * m + 2, :])
-        load_a(1)
+        load_a(0, 2)
+        load_a(2, 2)
         load_g(1)
         for b in (1, 2):
             nc.sync.dma_start(out=v_raw[b][:], in_=v_rows[b])
@@ -101,8 +104,8 @@ def tile_noise_error_backprop_e4_kernel(tc, g_words, g_scales, w, a, v, lam, gai
 
         v_words = [v_raw[b][:].rearrange("p a d -> p (a d)").bitcast(F32) for b in range(BLOCKS)]
         w_words = [w_raw[b][:].rearrange("p a c -> p (a c)").bitcast(F32) for b in range(BLOCKS)]
-        w_first_words = [w_first[g][:].rearrange("p a c -> p (a c)").bitcast(F32) for g in range(2)]
-        a_words = a_raw[:].rearrange("p i d -> p (i d)").bitcast(F32)
+        w_first_words = [w_first[s][:].bitcast(F32) for s in range(2)]
+        a_words = a_raw[:].rearrange("p m d -> p (m d)").bitcast(F32)
 
         def transposes(pieces):
             bank = psum.tile([P, 512], F32, name="bank", tag="tr", bufs=4)
@@ -112,10 +115,14 @@ def tile_noise_error_backprop_e4_kernel(tc, g_words, g_scales, w, a, v, lam, gai
                     nc.tensor.transpose(bank[:, (2 * j + u) * P : (2 * j + u + 1) * P], src, ident[:])
             return bank
 
-        def copy_out(bank, on_scalar):
+        def copy_out(bank, on_scalar, paired=False):
             grouped = work.tile([P, 1024], BF16, name="grouped", tag="grouped", bufs=8, align_bytes=64)
-            dst = grouped[:].bitcast(F32).rearrange("p (a r u) -> p a r u", a=2, u=2)
-            src = bank[:].rearrange("p (a u r) -> p a r u", a=2, u=2)
+            if paired:
+                dst = grouped[:].bitcast(F32).rearrange("p (r a u) -> p r a u", a=2, u=2)
+                src = bank[:].rearrange("p (a u r) -> p r a u", a=2, u=2)
+            else:
+                dst = grouped[:].bitcast(F32).rearrange("p (a r u) -> p a r u", a=2, u=2)
+                src = bank[:].rearrange("p (a u r) -> p a r u", a=2, u=2)
             if on_scalar:
                 nc.scalar.copy(out=dst, in_=src)
             else:
@@ -131,16 +138,24 @@ def tile_noise_error_backprop_e4_kernel(tc, g_words, g_scales, w, a, v, lam, gai
             return transposes([(v_perm[b], 256 * (2 * h + j), True) for j in range(2)])
 
         def w_tr(b, h, g):
-            if b == 0 and h == 0:
-                return transposes([(w_first_words[g], 256 * j, False) for j in range(2)])
             if b == 0:
                 return transposes([(w_words[b], 512 * (2 * h + j) + 256 * g, False) for j in range(2)])
             return transposes([(w_perm[b, h], 512 * j + 256 * g, True) for j in range(2)])
 
+        def first_tr(s):
+            return transposes([(w_first_words[s], 256 * g, False) for g in range(2)])
+
+        def first_q(s, grouped):
+            cols = slice(P * s, P * s + P)
+            for g in range(2):
+                nc.vector.quantize_mx(
+                    out=w_codes[0][g][:, cols].bitcast(E4M3),
+                    scales=w_sc[0][g][:, cols],
+                    in_=grouped[:, 512 * g : 512 * g + 512],
+                )
+
         def a_tr(m):
-            if m < 2:
-                return transposes([(a_words, 256 * (2 * m + j), False) for j in range(2)])
-            return transposes([(a_perm, 256 * (2 * (m - 2) + j), True) for j in range(2)])
+            return transposes([(a_perm[m // 2], 256 * (2 * (m % 2) + j), True) for j in range(2)])
 
         def v_q(b, h, grouped):
             cols = slice(256 * h, 256 * h + 256)
@@ -157,13 +172,15 @@ def tile_noise_error_backprop_e4_kernel(tc, g_words, g_scales, w, a, v, lam, gai
         def permute(dst, src, on_scalar):
             dst = dst.rearrange("p (x u q) -> p x u q", u=2, q=P)
             src = src.rearrange("p (x q u) -> p x u q", u=2, q=P)
-            if on_scalar:
-                nc.scalar.copy(out=dst, in_=src)
-            else:
-                nc.vector.tensor_copy(out=dst, in_=src)
+            n = dst.shape[1]
+            cut = {"scalar": n, "vector": 0, "both": n // 2}[on_scalar]
+            if cut > 0:
+                nc.scalar.copy(out=dst[:, :cut], in_=src[:, :cut])
+            if cut < n:
+                nc.vector.tensor_copy(out=dst[:, cut:], in_=src[:, cut:])
 
-        def a_permute(on_scalar):
-            permute(a_perm[:], a_words[:, 1024:2048], on_scalar)
+        def a_permute(h, on_scalar):
+            permute(a_perm[h][:], a_words[:, 1024 * h : 1024 * h + 1024], on_scalar)
 
         def v_permute(b, on_scalar):
             permute(v_perm[b][:], v_words[b], on_scalar)
@@ -205,19 +222,18 @@ def tile_noise_error_backprop_e4_kernel(tc, g_words, g_scales, w, a, v, lam, gai
 
         def finish(b, i):
             res = work.tile([P, NB], F32, name="res", tag="res", bufs=24)
-            pieces = 2 if (b, i) == (BLOCKS - 1, TILES - 1) else 1
-            n = P // pieces
-            for s in range(pieces):
-                cols = slice(4 * n * s, 4 * n * (s + 1))
+            cuts = (0, 96, P) if (b, i) == (BLOCKS - 1, TILES - 1) else (0, P)
+            for lo, hi in zip(cuts, cuts[1:]):
+                cols = slice(4 * lo, 4 * hi)
                 nc.vector.scalar_tensor_tensor(
                     out=res[:, cols].rearrange("m (p a) -> m p a", a=4),
-                    in0=accs[b, i][:].rearrange("m (a p) -> m p a", a=4)[:, n * s : n * (s + 1), :],
+                    in0=accs[b, i][:].rearrange("m (a p) -> m p a", a=4)[:, lo:hi, :],
                     scalar=lam_sb[:, i : i + 1],
                     in1=gain_sb[b][:, cols].rearrange("m (p a) -> m p a", a=4),
                     op0=MULT,
                     op1=MULT,
                 )
-                nc.sync.dma_start(out=out[P * i : P * i + P, NB * b + 4 * n * s : NB * b + 4 * n * (s + 1)], in_=res[:, cols])
+                nc.sync.dma_start(out=out[P * i : P * i + P, NB * b + 4 * lo : NB * b + 4 * hi], in_=res[:, cols])
 
         def gain_spread(b):
             bank = psum.tile([P, NB], BF16, name="gain_bank", tag="tr", bufs=4)
@@ -226,52 +242,74 @@ def tile_noise_error_backprop_e4_kernel(tc, g_words, g_scales, w, a, v, lam, gai
                 nc.tensor.transpose(bank[:, P * j : P * j + P], gain_cols[:, m : m + 1].to_broadcast([P, P]), ident_bf[:])
             nc.scalar.copy(out=gain_sb[b][:], in_=bank[:])
 
-        def copies(banks, on_scalar):
-            return [copy_out(bank, s) for bank, s in zip(banks, on_scalar)]
+        def copies(banks, on_scalar, paired=False):
+            return [copy_out(bank, s, paired) for bank, s in zip(banks, on_scalar)]
 
         def tile_av_first(b, i):
-            open_acc(b, i)
-            av(b, i, True, False)
+            paired = (b, i) < (BLOCKS - 1, TILES - 2)
+            ahead = (i, i + 1) if i % 2 == 0 else ()
+            for j in ahead if paired else (i,):
+                open_acc(b, j)
+                av(b, j, True, False)
             gw(b, i, False, True)
             finish(b, i)
 
-        w00 = copies([w_tr(0, 0, 0), w_tr(0, 0, 1)], [False, False])
+        warm_bank = psum.tile([P, NB], F32, name="warm_bank", tag="acc", bufs=4)
+
+        def warm(passes):
+            for k in range(passes):
+                nc.tensor.matmul_mx(
+                    out=warm_bank[:],
+                    lhsT=warm_codes[:, 0:P].bitcast(E4M3),
+                    lhsT_scale=warm_sc[:, 0:P],
+                    rhs=warm_codes[:].bitcast(E4M3),
+                    rhs_scale=warm_sc[:],
+                    start=True,
+                    stop=True,
+                )
+
+        warm(3)
+        w00 = copies([first_tr(0), first_tr(1)], [True, True])
+        first_q(0, w00[0])
+        first_q(1, w00[1])
+        warm(1)
+        w01 = copies([w_tr(0, 1, 0), w_tr(0, 1, 1)], [True, True])
         vec_bank = psum.tile([P, P], BF16, name="vec_bank", tag="tr", bufs=4)
         nc.tensor.transpose(vec_bank[:], vec[:], ident_bf[:])
-        nc.scalar.copy(out=gain_cols[:], in_=vec_bank[:, 8:20])
-        nc.scalar.copy(out=lam_sb[:], in_=vec_bank[:, 0:8])
-        w01 = copies([w_tr(0, 1, 0), w_tr(0, 1, 1)], [True, False])
-        w_q(0, 0, 0, w00[0])
-        w_q(0, 0, 1, w00[1])
-        gain_spread(0)
+        warm(1)
         w_q(0, 1, 0, w01[0])
         w_q(0, 1, 1, w01[1])
-        v0 = copies([v_tr(0, 0), v_tr(0, 1)], [False, True])
-        v_q(0, 0, v0[0])
-        a0 = copies([a_tr(0), a_tr(1)], [True, False])
-        v_q(0, 1, v0[1])
-        open_acc(0, 0)
-        gw(0, 0, True, False)
-        a_permute(True)
-        a_q(0, a0[0])
-        gain_spread(1)
-        gain_spread(2)
-        a_q(1, a0[1])
-        a1 = copies([a_tr(2), a_tr(3)], [True, True])
-        for i in range(1, 4):
+        nc.scalar.copy(out=gain_cols[:], in_=vec_bank[:, 8:20])
+        nc.scalar.copy(out=lam_sb[:], in_=vec_bank[:, 0:8])
+        v0 = copies([v_tr(0, 0), v_tr(0, 1)], [True, False])
+        warm(0)
+        for i in range(3):
             open_acc(0, i)
             gw(0, i, True, False)
-        v_permute(1, True)
-        w_permute(1, 0, False)
+        v_q(0, 0, v0[0])
+        v_q(0, 1, v0[1])
+        a_permute(0, "scalar")
+        a_permute(1, "both")
+        a0 = copies([a_tr(0), a_tr(1)], [True, False], True)
+        gain_spread(0)
+        a_q(0, a0[0])
+        a_q(1, a0[1])
+        a1 = copies([a_tr(2), a_tr(3)], [True, True], True)
+        gain_spread(1)
+        for i in range(3, 4):
+            open_acc(0, i)
+            gw(0, i, True, False)
+        v_permute(1, "vector")
+        w_permute(1, 0, "scalar")
+        w_permute(1, 1, "scalar")
         for i in range(4):
             av(0, i, False, True)
             finish(0, i)
             if i < 2:
                 a_q(2 + i, a1[i])
         vg = copies([v_tr(1, 0), v_tr(1, 1)], [True, True])
-        wg = copies([w_tr(1, 0, g) for g in range(2)], [True, False])
-        w_permute(1, 1, True)
-        v_permute(2, False)
+        wg = copies([w_tr(1, 0, g) for g in range(2)], [False, True])
+        v_permute(2, "both")
         tile_av_first(0, 4)
         v_q(1, 0, vg[0])
         v_q(1, 1, vg[1])
@@ -280,8 +318,8 @@ def tile_noise_error_backprop_e4_kernel(tc, g_words, g_scales, w, a, v, lam, gai
             w_q(1, 0, g, wg[g])
         wg = copies([w_tr(1, 1, g) for g in range(2)], [True, True])
         vg = copies([v_tr(2, 0), v_tr(2, 1)], [True, True])
-        w_permute(2, 0, False)
-        w_permute(2, 1, False)
+        w_permute(2, 0, "vector")
+        w_permute(2, 1, "scalar")
         tile_av_first(0, 6)
         for g in range(2):
             w_q(1, 1, g, wg[g])
@@ -289,6 +327,7 @@ def tile_noise_error_backprop_e4_kernel(tc, g_words, g_scales, w, a, v, lam, gai
         for h in range(2):
             v_q(2, h, vg[h])
 
+        gain_spread(2)
         wb = [w_tr(2, h, g) for h in range(2) for g in range(2)]
         wg = copies(wb, [True] * 4)
         tile_av_first(1, 0)

from contextlib import ExitStack

import concourse.mybir as mybir
from concourse.masks import make_identity

T, H, C, D = 1024, 1536, 1024, 512
FLOPS = 2 * T * H * (C + D)

F32 = mybir.dt.float32
BF16 = mybir.dt.bfloat16
I32 = mybir.dt.int32
U32 = mybir.dt.uint32
U8 = mybir.dt.uint8
E4M3 = mybir.dt.float8_e4m3fn_x4
E5M2 = mybir.dt.float8_e5m2_x4
MULT = mybir.AluOpType.mult
COPY = mybir.ActivationFunctionType.Copy

P = 128
NB = 512
BLOCKS = H // NB
TILES = T // P


def tile_noise_error_backprop_e4_kernel(tc, g_words, g_scales, w, a, v, lam, gain, out):
    nc = tc.nc
    with ExitStack() as ctx:
        keep = ctx.enter_context(tc.tile_pool(name="keep", bufs=1))
        work = ctx.enter_context(tc.tile_pool(name="work", bufs=1))
        psum = ctx.enter_context(tc.psum_pool(name="psum", bufs=1))
        ctx.enter_context(tc.manual_schedule())

        vec = keep.tile([P, P], BF16, name="vec")
        ident = keep.tile([P, P], F32, name="ident")
        ident_bf = keep.tile([P, P], BF16, name="ident_bf")
        lam_sb = keep.tile([P, TILES], F32, name="lam_sb")
        gain_cols = keep.tile([P, H // P], BF16, name="gain_cols")
        gain_sb = [keep.tile([P, NB], BF16, name="gain_sb%d" % b) for b in range(BLOCKS)]
        dummy = keep.tile([P, 1], F32, name="dummy")
        g_raw = [keep.tile([P, 2, T // 2], U32, name="g_raw%d" % h, align_bytes=64) for h in range(2)]
        g_sc = keep.tile([P, 2, T], U8, name="g_sc", align_bytes=64)
        a_raw = keep.tile([P, TILES // 2, 2 * D], BF16, name="a_raw", align_bytes=64)
        a_codes = keep.tile([P, T], U32, name="a_codes", align_bytes=64)
        a_sc = keep.tile([P, T], U8, name="a_sc", align_bytes=64)
        v_raw = [keep.tile([P, 4, D], BF16, name="v_raw%d" % b, align_bytes=64) for b in range(BLOCKS)]
        w_first = [keep.tile([P, C], BF16, name="w_first%d" % s, align_bytes=64) for s in range(2)]
        w_raw = [keep.tile([P, 4, C], BF16, name="w_raw%d" % b, align_bytes=64) for b in range(BLOCKS)]
        v_codes = [keep.tile([P, NB], U32, name="v_codes%d" % b, align_bytes=64) for b in range(BLOCKS)]
        v_sc = [keep.tile([P, NB], U8, name="v_sc%d" % b, align_bytes=64) for b in range(BLOCKS)]
        w_codes = [[keep.tile([P, NB], U32, name="w_codes%d_%d" % (b, g), align_bytes=64) for g in range(2)] for b in range(BLOCKS)]
        w_sc = [[keep.tile([P, NB], U8, name="w_sc%d_%d" % (b, g), align_bytes=64) for g in range(2)] for b in range(BLOCKS)]
        v_perm = {b: keep.tile([P, 4 * D // 2], F32, name="v_perm%d" % b, align_bytes=64) for b in (1, 2)}
        a_perm = [keep.tile([P, 4 * D // 2], F32, name="a_perm%d" % h, align_bytes=64) for h in range(2)]
        w_perm = {(b, h): keep.tile([P, 2 * C // 2], F32, name="w_perm%d_%d" % (b, h), align_bytes=64) for b in (1, 2) for h in range(2)}

        warm_in = keep.tile([P, 4 * NB], BF16, name="warm_in", align_bytes=64)
        warm_codes = keep.tile([P, NB], U32, name="warm_codes", align_bytes=64)
        warm_sc = keep.tile([P, NB], U8, name="warm_sc", align_bytes=64)
        nc.vector.memset(dummy[:], 0.0)
        nc.vector.memset(warm_in[:].bitcast(F32), 0.0)
        nc.gpsimd.memset(vec[:], 0.0)
        nc.vector.quantize_mx(out=warm_codes[:].bitcast(E4M3), scales=warm_sc[:], in_=warm_in[:])
        nc.vector.memset(g_sc[:].rearrange("p g n -> p (g n)").bitcast(I32), 0)
        make_identity(nc, ident[:])
        nc.scalar.dma_start(out=vec[0:8, :], in_=lam.rearrange("(r c) -> r c", c=P))
        gain_rows = gain.rearrange("(r c) -> r c", c=P)
        nc.scalar.dma_start(out=vec[8:16, :], in_=gain_rows[0:8, :])
        nc.scalar.dma_start(out=vec[16:20, :], in_=gain_rows[8:12, :])
        nc.scalar.copy(out=dummy[:], in_=dummy[:])
        nc.vector.tensor_copy(out=ident_bf[:], in_=ident[:])

        a_rows = a.rearrange("(m p j) d -> p m (j d)", p=P, j=2)
        v_rows = v.rearrange("(b p a) d -> b p a d", b=BLOCKS, a=4)
        w_rows = w.rearrange("(b p a) c -> b p a c", b=BLOCKS, a=4)
        g_bytes = g_words.rearrange("g p n t -> p g (n t)")

        def load_a(m, n):
            nc.sync.dma_start(out=a_raw[:, m : m + n, :], in_=a_rows[:, m : m + n, :])

        def load_g(h):
            bytes_ = slice(h * 2048, h * 2048 + 2048)
            nc.sync.dma_start(out=g_raw[h][:].bitcast(I32), in_=g_bytes[:, :, bytes_].bitcast(I32))

        def load_w(b, h):
            nc.sync.dma_start(out=w_raw[b][:, 2 * h : 2 * h + 2, :], in_=w_rows[b, :, 2 * h : 2 * h + 2, :])

        for s in range(2):
            nc.sync.dma_start(out=w_first[s][:], in_=w_rows[0, :, s, :])
        load_w(0, 1)
        nc.sync.dma_start(out=v_raw[0][:], in_=v_rows[0])
        for q in range(4):
            nc.sync.dma_start(
                out=g_sc[32 * q : 32 * q + 4, :, :].bitcast(I32),
                in_=g_scales[:, 4 * q : 4 * q + 4, :].rearrange("g r n -> r g n").bitcast(I32),
            )
        load_g(0)
        load_a(0, 2)
        load_a(2, 2)
        load_g(1)
        for b in (1, 2):
            nc.sync.dma_start(out=v_raw[b][:], in_=v_rows[b])
            load_w(b, 0)
            load_w(b, 1)

        v_words = [v_raw[b][:].rearrange("p a d -> p (a d)").bitcast(F32) for b in range(BLOCKS)]
        w_words = [w_raw[b][:].rearrange("p a c -> p (a c)").bitcast(F32) for b in range(BLOCKS)]
        w_first_words = [w_first[s][:].bitcast(F32) for s in range(2)]
        a_words = a_raw[:].rearrange("p m d -> p (m d)").bitcast(F32)

        def transposes(pieces):
            bank = psum.tile([P, 512], F32, name="bank", tag="tr", bufs=4)
            for j, (words, start, permuted) in enumerate(pieces):
                for u in range(2):
                    src = words[:, start + 128 * u : start + 128 * u + 128] if permuted else words[:, start + u : start + 256 : 2]
                    nc.tensor.transpose(bank[:, (2 * j + u) * P : (2 * j + u + 1) * P], src, ident[:])
            return bank

        def copy_out(bank, on_scalar, paired=False):
            grouped = work.tile([P, 1024], BF16, name="grouped", tag="grouped", bufs=8, align_bytes=64)
            if paired:
                dst = grouped[:].bitcast(F32).rearrange("p (r a u) -> p r a u", a=2, u=2)
                src = bank[:].rearrange("p (a u r) -> p r a u", a=2, u=2)
            else:
                dst = grouped[:].bitcast(F32).rearrange("p (a r u) -> p a r u", a=2, u=2)
                src = bank[:].rearrange("p (a u r) -> p a r u", a=2, u=2)
            if on_scalar:
                nc.scalar.copy(out=dst, in_=src)
            else:
                nc.vector.tensor_copy(out=dst, in_=src)
            return grouped

        def quantise(grouped, codes, scales):
            nc.vector.quantize_mx(out=codes.bitcast(E4M3), scales=scales, in_=grouped[:])

        def v_tr(b, h):
            if b == 0:
                return transposes([(v_words[b], 256 * (2 * h + j), False) for j in range(2)])
            return transposes([(v_perm[b], 256 * (2 * h + j), True) for j in range(2)])

        def w_tr(b, h, g):
            if b == 0:
                return transposes([(w_words[b], 512 * (2 * h + j) + 256 * g, False) for j in range(2)])
            return transposes([(w_perm[b, h], 512 * j + 256 * g, True) for j in range(2)])

        def first_tr(s):
            return transposes([(w_first_words[s], 256 * g, False) for g in range(2)])

        def first_q(s, grouped):
            cols = slice(P * s, P * s + P)
            for g in range(2):
                nc.vector.quantize_mx(
                    out=w_codes[0][g][:, cols].bitcast(E4M3),
                    scales=w_sc[0][g][:, cols],
                    in_=grouped[:, 512 * g : 512 * g + 512],
                )

        def a_tr(m):
            return transposes([(a_perm[m // 2], 256 * (2 * (m % 2) + j), True) for j in range(2)])

        def v_q(b, h, grouped):
            cols = slice(256 * h, 256 * h + 256)
            quantise(grouped, v_codes[b][:, cols], v_sc[b][:, cols])

        def w_q(b, h, g, grouped):
            cols = slice(256 * h, 256 * h + 256)
            quantise(grouped, w_codes[b][g][:, cols], w_sc[b][g][:, cols])

        def a_q(m, grouped):
            cols = slice(256 * m, 256 * m + 256)
            quantise(grouped, a_codes[:, cols], a_sc[:, cols])

        def permute(dst, src, on_scalar):
            dst = dst.rearrange("p (x u q) -> p x u q", u=2, q=P)
            src = src.rearrange("p (x q u) -> p x u q", u=2, q=P)
            n = dst.shape[1]
            cut = {"scalar": n, "vector": 0, "both": n // 2}[on_scalar]
            if cut > 0:
                nc.scalar.copy(out=dst[:, :cut], in_=src[:, :cut])
            if cut < n:
                nc.vector.tensor_copy(out=dst[:, cut:], in_=src[:, cut:])

        def a_permute(h, on_scalar):
            permute(a_perm[h][:], a_words[:, 1024 * h : 1024 * h + 1024], on_scalar)

        def v_permute(b, on_scalar):
            permute(v_perm[b][:], v_words[b], on_scalar)

        def w_permute(b, h, on_scalar):
            permute(w_perm[b, h][:], w_words[b][:, 1024 * h : 1024 * h + 1024], on_scalar)

        accs = {}

        def open_acc(b, i):
            acc = psum.tile([P, NB], F32, name="acc", tag="acc", bufs=4)
            accs[b, i] = acc

        def av(b, i, start, stop):
            rows = slice(P * i, P * i + P)
            nc.tensor.matmul_mx(
                out=accs[b, i][:],
                lhsT=a_codes[:, rows].bitcast(E4M3),
                lhsT_scale=a_sc[:, rows],
                rhs=v_codes[b][:].bitcast(E4M3),
                rhs_scale=v_sc[b][:],
                start=start,
                stop=stop,
            )

        def gw(b, i, start, stop):
            rows = slice(P * i, P * i + P)
            words = slice(P * (i % 4), P * (i % 4) + P)
            for g in range(2):
                nc.tensor.matmul_mx(
                    out=accs[b, i][:],
                    lhsT=g_raw[i // 4][:, g, words].bitcast(E5M2),
                    lhsT_scale=g_sc[:, g, rows],
                    rhs=w_codes[b][g][:].bitcast(E4M3),
                    rhs_scale=w_sc[b][g][:],
                    start=start and g == 0,
                    stop=stop and g == 1,
                )

        def finish(b, i):
            res = work.tile([P, NB], F32, name="res", tag="res", bufs=24)
            cuts = (0, 96, P) if (b, i) == (BLOCKS - 1, TILES - 1) else (0, P)
            for lo, hi in zip(cuts, cuts[1:]):
                cols = slice(4 * lo, 4 * hi)
                nc.vector.scalar_tensor_tensor(
                    out=res[:, cols].rearrange("m (p a) -> m p a", a=4),
                    in0=accs[b, i][:].rearrange("m (a p) -> m p a", a=4)[:, lo:hi, :],
                    scalar=lam_sb[:, i : i + 1],
                    in1=gain_sb[b][:, cols].rearrange("m (p a) -> m p a", a=4),
                    op0=MULT,
                    op1=MULT,
                )
                nc.sync.dma_start(out=out[P * i : P * i + P, NB * b + 4 * lo : NB * b + 4 * hi], in_=res[:, cols])

        def gain_spread(b):
            bank = psum.tile([P, NB], BF16, name="gain_bank", tag="tr", bufs=4)
            for j in range(4):
                m = 4 * b + j
                nc.tensor.transpose(bank[:, P * j : P * j + P], gain_cols[:, m : m + 1].to_broadcast([P, P]), ident_bf[:])
            nc.scalar.copy(out=gain_sb[b][:], in_=bank[:])

        def copies(banks, on_scalar, paired=False):
            return [copy_out(bank, s, paired) for bank, s in zip(banks, on_scalar)]

        def tile_av_first(b, i):
            paired = (b, i) < (BLOCKS - 1, TILES - 2)
            ahead = (i, i + 1) if i % 2 == 0 else ()
            for j in ahead if paired else (i,):
                open_acc(b, j)
                av(b, j, True, False)
            gw(b, i, False, True)
            finish(b, i)

        warm_bank = psum.tile([P, NB], F32, name="warm_bank", tag="acc", bufs=4)

        def warm(passes):
            for k in range(passes):
                nc.tensor.matmul_mx(
                    out=warm_bank[:],
                    lhsT=warm_codes[:, 0:P].bitcast(E4M3),
                    lhsT_scale=warm_sc[:, 0:P],
                    rhs=warm_codes[:].bitcast(E4M3),
                    rhs_scale=warm_sc[:],
                    start=True,
                    stop=True,
                )

        warm(3)
        w00 = copies([first_tr(0), first_tr(1)], [True, True])
        first_q(0, w00[0])
        first_q(1, w00[1])
        warm(1)
        w01 = copies([w_tr(0, 1, 0), w_tr(0, 1, 1)], [True, True])
        vec_bank = psum.tile([P, P], BF16, name="vec_bank", tag="tr", bufs=4)
        nc.tensor.transpose(vec_bank[:], vec[:], ident_bf[:])
        warm(1)
        w_q(0, 1, 0, w01[0])
        w_q(0, 1, 1, w01[1])
        nc.scalar.copy(out=gain_cols[:], in_=vec_bank[:, 8:20])
        nc.scalar.copy(out=lam_sb[:], in_=vec_bank[:, 0:8])
        v0 = copies([v_tr(0, 0), v_tr(0, 1)], [True, False])
        warm(0)
        for i in range(3):
            open_acc(0, i)
            gw(0, i, True, False)
        v_q(0, 0, v0[0])
        v_q(0, 1, v0[1])
        a_permute(0, "scalar")
        a_permute(1, "both")
        a0 = copies([a_tr(0), a_tr(1)], [True, False], True)
        gain_spread(0)
        a_q(0, a0[0])
        a_q(1, a0[1])
        a1 = copies([a_tr(2), a_tr(3)], [True, True], True)
        gain_spread(1)
        for i in range(3, 4):
            open_acc(0, i)
            gw(0, i, True, False)
        v_permute(1, "vector")
        w_permute(1, 0, "scalar")
        w_permute(1, 1, "scalar")
        for i in range(4):
            av(0, i, False, True)
            finish(0, i)
            if i < 2:
                a_q(2 + i, a1[i])
        vg = copies([v_tr(1, 0), v_tr(1, 1)], [True, True])
        wg = copies([w_tr(1, 0, g) for g in range(2)], [False, True])
        v_permute(2, "both")
        tile_av_first(0, 4)
        v_q(1, 0, vg[0])
        v_q(1, 1, vg[1])
        tile_av_first(0, 5)
        for g in range(2):
            w_q(1, 0, g, wg[g])
        wg = copies([w_tr(1, 1, g) for g in range(2)], [True, True])
        vg = copies([v_tr(2, 0), v_tr(2, 1)], [True, True])
        w_permute(2, 0, "vector")
        w_permute(2, 1, "scalar")
        tile_av_first(0, 6)
        for g in range(2):
            w_q(1, 1, g, wg[g])
        tile_av_first(0, 7)
        for h in range(2):
            v_q(2, h, vg[h])

        gain_spread(2)
        wb = [w_tr(2, h, g) for h in range(2) for g in range(2)]
        wg = copies(wb, [True] * 4)
        tile_av_first(1, 0)
        tile_av_first(1, 1)
        for g in range(2):
            w_q(2, 0, g, wg[g])
        tile_av_first(1, 2)
        for g in range(2):
            w_q(2, 1, g, wg[2 + g])
        for i in range(3, TILES):
            tile_av_first(1, i)

        for i in range(TILES):
            tile_av_first(2, i)
